import numpy as np
import ml_dtypes


def mxq(x, axis, fmt="e4m3"):
    dtype, down = {"e4m3": (ml_dtypes.float8_e4m3fn, 7), "e5m2": (ml_dtypes.float8_e5m2, 14)}[fmt]
    v = np.moveaxis(np.asarray(x, np.float32).astype(ml_dtypes.bfloat16).astype(np.float64), axis, -1)
    blocks = v.reshape(v.shape[:-1] + (-1, 32))
    amax = np.abs(blocks).max(-1, keepdims=True)
    byte = np.maximum(np.where(amax > 0, np.frexp(amax)[1] - 1 + 127, 0) - down, 1)
    scale = np.exp2(byte - 127.0)
    codes = (blocks / scale).astype(np.float32).astype(dtype).astype(np.float64)
    return np.moveaxis((codes * scale).reshape(v.shape), -1, axis)


WIDE = False


def mx_kscale(k):
    if not WIDE:
        return np.ones(k)
    levels = np.array([10, -10, 5, -5, 0])
    if k % 512:
        return np.exp2(np.random.permutation(np.resize(levels, k // 32))).repeat(32)
    a = np.empty((k // 512, 16))
    for p in range(k // 512):
        a[p, :8] = np.random.permutation(np.resize(levels, 8))
        for g in range(8):
            far = levels[np.abs(levels - a[p, g]) >= 10]
            a[p, g + 8] = far[np.random.randint(len(far))]
    return np.exp2(a.ravel()).repeat(32)


def f64(x):
    return np.asarray(x).astype(np.float64)


def striped8(idx):
    return np.asarray(idx).reshape(8, -1, 16).transpose(0, 2, 1).reshape(128, -1).astype(np.uint16)


def unstriped8(offs):
    return offs.reshape(8, 16, -1).transpose(0, 2, 1).reshape(8, -1).astype(np.int64)


def pick8(x, idx, run):
    r = np.arange(len(x))
    return x[r[:, None], idx[r % (8 * run) // run]]


E2M1 = np.array([0.0, 0.5, 1.0, 1.5, 2.0, 3.0, 4.0, 6.0, -0.0, -0.5, -1.0, -1.5, -2.0, -3.0, -4.0, -6.0])


def pack_weight(w, fmt):
    k, n = w.shape
    w = f64(np.asarray(w, np.float32).astype(ml_dtypes.bfloat16)).reshape(k // 32, 32, n)
    amax = np.abs(w).max(1)
    if fmt == "e4m3":
        byte = np.frexp(amax)[1] - 1 + 127 - 7
    else:
        mant, ex = np.frexp(amax / 6.0)
        byte = np.where(mant > 0.5, ex, ex - 1) + 127
    byte = np.clip(np.where(amax > 0, byte, 1), 1, 254)
    scaled = (w * np.exp2(127.0 - byte)[:, None, :]).reshape(k, n).astype(np.float32)
    by_word = np.ascontiguousarray(scaled.reshape(k // 512, 128, 4, n).transpose(0, 1, 3, 2))
    if fmt == "e4m3":
        words = by_word.astype(ml_dtypes.float8_e4m3fn).view(np.uint8)
    else:
        c = by_word.astype(ml_dtypes.float4_e2m1fn).view(np.uint8) & 0xF
        words = (c[..., 0::2] | (c[..., 1::2] << 4)).reshape(k // 512, 128, 2 * n)
    return np.ascontiguousarray(words), np.ascontiguousarray(byte.astype(np.uint8).reshape(k // 512, 16, n))


def unpack_weight(words, scales, fmt):
    g, _, n = scales.shape
    words = np.ascontiguousarray(words).reshape(g, 128, n, -1)
    if fmt == "e4m3":
        vals = words.view(ml_dtypes.float8_e4m3fn).astype(np.float64)
    else:
        nib = np.empty((g, 128, n, 4), np.uint8)
        nib[..., 0::2] = words & 0xF
        nib[..., 1::2] = words >> 4
        vals = E2M1[nib]
    vals = vals * np.repeat(np.exp2(scales.astype(np.float64) - 127.0), 8, axis=1)[..., None]
    return vals.transpose(0, 1, 3, 2).reshape(g * 512, n)


def sigmoid(v):
    return 1.0 / (1.0 + np.exp(-v))


D, E, T, Q, I = 512, 512, 1024, 128, 512


def setup_inputs():
    n = np.random.standard_normal
    idx = np.stack([np.random.permutation(T)[:I] for _ in range(8)])
    fd = mx_kscale(D)
    fe = mx_kscale(E)
    keysp = pack_weight(n((D, T)) / fd[:, None], "e4m3")
    return {
        "query": (n((D, Q)) * 0.4 / np.sqrt(D) * fd[:, None]).astype(np.float32),
        "keys_words": keysp[0],
        "keys_scales": keysp[1],
        "gout": (n((E, Q)) * 1 / np.sqrt(E) * fe[:, None]).astype(np.float32),
        "vals": (n((E, T)) / fe[:, None]).astype(np.float32),
        "steep": (np.random.uniform(2.0, 5.0, (Q, 1))).astype(np.float32),
        "boost": (np.random.uniform(0.5, 2.0, (1, I))).astype(np.float32),
        "fac": (np.random.uniform(0.5, 2.0, (1, T))).astype(np.float32),
        "dquery": (n((D, Q)) * 1.0 / np.sqrt(D) * fd[:, None]).astype(np.float32),
        "base": (0.5 * n((Q, T))).astype(np.float32),
        "offs": striped8(idx),
    }


def reference(query, keys_words, keys_scales, gout, vals, steep, boost, fac, dquery, base, offs):
    idx = unstriped8(offs)
    keysu = unpack_weight(keys_words, keys_scales, "e4m3")
    queryq = mxq(f64(query), 0, "e4m3")
    a = queryq.T @ keysu
    dqueryq = mxq(f64(dquery), 0, "e4m3")
    ta = dqueryq.T @ keysu
    b = sigmoid(pick8(a, idx, 16) * f64(steep))
    bb = b * f64(boost)
    bf = np.zeros((Q, T))
    bf[np.arange(Q)[:, None], idx[np.arange(Q) % 128 // 16]] = bb
    s = a + bf
    p = np.exp(s - np.max(s, axis=1, keepdims=True))
    z = np.sum(p, axis=1, keepdims=True)
    goutq = mxq(f64(gout), 0, "e4m3")
    valsq = mxq(f64(vals), 0, "e4m3")
    c0 = goutq.T @ valsq
    dz = np.sum(c0 * p * f64(fac) / np.square(z) * (-1.0), axis=1, keepdims=True)
    dp = c0 / z * f64(fac) + dz
    ds = dp * p
    dbb = pick8(ds, idx, 16)
    db = dbb * f64(boost)
    xb = pick8(ta, idx, 16) * f64(steep) * b * (1.0 - b)
    xbb = xb * f64(boost)
    xbf = np.zeros((Q, T))
    xbf[np.arange(Q)[:, None], idx[np.arange(Q) % 128 // 16]] = xbb
    xs = ta + xbf
    xp = xs * p
    xz = np.sum(xp, axis=1, keepdims=True)
    xdz = np.sum((xp * f64(fac) * c0 - xz * z * 2.0 * c0 * p * f64(fac) / np.square(z)) / np.square(z) * (-1.0), axis=1, keepdims=True)
    xdp = xz * c0 / np.square(z) * (-1.0) * f64(fac) + xdz
    xds = xdp * p + xp * dp
    xdbb = pick8(xds, idx, 16)
    xdb = xdbb * f64(boost)
    xe1 = ((xdb * b + xb * db) * (1.0 - b) + xb * (-1.0) * db * b) * f64(steep)
    xs1 = np.zeros((Q, T))
    xs1[np.arange(Q)[:, None], idx[np.arange(Q) % 128 // 16]] = xe1
    xda = xds + xs1
    y = xda * 1024.0 + f64(base)
    return y

@@ -1,0 +1,281 @@
+from contextlib import ExitStack
+
+import concourse.mybir as mybir
+from concourse.masks import make_identity
+
+F32 = mybir.dt.float32
+BF16 = mybir.dt.bfloat16
+I32 = mybir.dt.int32
+U32 = mybir.dt.uint32
+U16 = mybir.dt.uint16
+U8 = mybir.dt.uint8
+FP8X4 = mybir.dt.float8_e4m3fn_x4
+ALU = mybir.AluOpType
+ACT = mybir.ActivationFunctionType
+AXIS = mybir.AxisListType
+
+P = 128
+PACK = 4
+D, E, T, Q, I = 512, 512, 1024, 128, 512
+BANK = 512
+HALVES = T // BANK
+BLOCKS = T // P
+PER_BANK = BANK // P
+CHUNK = 256
+CHUNKS = T // CHUNK
+GAIN = 1024.0
+STORES = 4
+RUNS = 2
+
+FLOPS = 3 * 2 * 512 * Q * T
+
+
+def tile_attend_hvboost_heads_kernel(tc, query, keys_words, keys_scales, gout, vals, steep, boost, fac, dquery, base, offs, out):
+    nc = tc.nc
+    with ExitStack() as ctx:
+        sb = ctx.enter_context(tc.tile_pool(name="sb", bufs=1))
+        ps = ctx.enter_context(tc.psum_pool(name="ps", bufs=1))
+
+        def tile(name, shape, dtype=F32):
+            return sb.tile(shape, dtype, name=name, align_bytes=64)
+
+        def bank(name, tag):
+            return ps.tile([P, BANK], F32, name=name, tag=tag)
+
+        def half(h):
+            return slice(h * BANK, (h + 1) * BANK)
+
+        def block(j):
+            return slice(j * P, (j + 1) * P)
+
+        def run(r):
+            return slice(r * I // RUNS, (r + 1) * I // RUNS)
+
+        def run_cols(r):
+            return slice(r * I // RUNS // 16, (r + 1) * I // RUNS // 16)
+
+        offsets = sb.tile([P, I // 16], U16, name="offsets")
+
+        key_scales = tile("key_scales", [P, T], U8)
+        nc.gpsimd.memset(key_scales[:].bitcast(I32), 0)
+        fac_rows = tile("fac_rows", [P, P])
+        nc.vector.memset(fac_rows[:], 0.0)
+        warm = tile("warm", [P, 8])
+        nc.vector.memset(warm[:], 0.0)
+        bf = tile("bf", [P, T])
+        xbf = tile("xbf", [P, T])
+        xs1 = tile("xs1", [P, T])
+        for w_ in (bf, xbf, xs1):
+            nc.vector.memset(w_[:], 0.0)
+
+        def load_rows(name, src, width):
+            raw = tile(name, [P, PACK, width])
+            nc.sync.dma_start(out=raw[:], in_=src.rearrange("(p j) w -> p j w", j=PACK))
+            return raw
+
+        boost_cols = tile("boost_cols", [P, PACK])
+        nc.scalar.dma_start(out=boost_cols[:], in_=boost.rearrange("o (p c) -> p (o c)", c=PACK))
+        steep_col = tile("steep_col", [P, 1])
+        nc.scalar.dma_start(out=steep_col[:], in_=steep)
+
+        q_raw = load_rows("q_raw", query, Q)
+        key_words = tile("key_words", [P, T], U32)
+        nc.sync.dma_start(out=key_words[:].bitcast(I32), in_=keys_words[0].rearrange("p n t -> p (n t)").bitcast(I32))
+        for quad in range(4):
+            nc.scalar.dma_start(
+                out=key_scales[32 * quad : 32 * quad + 4, :].bitcast(I32),
+                in_=keys_scales[0, 4 * quad : 4 * quad + 4, :].bitcast(I32),
+            )
+        nc.sync.dma_start(offsets[:], offs)
+        dq_raw = load_rows("dq_raw", dquery, Q)
+        v_raw = [load_rows("v_raw%d" % c, vals[:, c * CHUNK : (c + 1) * CHUNK], CHUNK) for c in range(2)]
+        g_raw = load_rows("g_raw", gout, Q)
+        v_raw = v_raw + [load_rows("v_raw%d" % c, vals[:, c * CHUNK : (c + 1) * CHUNK], CHUNK) for c in range(2, CHUNKS)]
+        nc.sync.dma_start(out=fac_rows[0:BLOCKS, :], in_=fac.rearrange("o (j p) -> (o j) p", p=P))
+        base_sb = tile("base_sb", [P, T])
+        nc.sync.dma_start(out=base_sb[:], in_=base)
+
+        ident = tile("ident", [P, P])
+        make_identity(nc, ident[:])
+
+        warm_out = tile("warm_out", [P, 8])
+        nc.scalar.activation(warm_out[:, 0:1], warm[:, 0:1], ACT.Tanh)
+
+        def interleave(copy, name, raw, width):
+            grouped = tile(name, [P, width, PACK], BF16)
+            copy(
+                out=grouped[:].rearrange("p (c i) j -> p c j i", i=4),
+                in_=raw[:].rearrange("p j (c i) -> p c j i", i=4),
+            )
+            return grouped
+
+        def quantize(name, grouped, width):
+            codes = tile(name + "_codes", [P, width], U32)
+            scales = tile(name + "_scales", [P, width], U8)
+            nc.vector.quantize_mx(out=codes[:].bitcast(FP8X4), scales=scales[:], in_=grouped[:].rearrange("p w j -> p (w j)"))
+            return codes, scales
+
+        def score(name, tag, codes, scales):
+            banks = []
+            for h in range(HALVES):
+                acc = bank("%s%d" % (name, h), "%s%d" % (tag, h))
+                nc.tensor.matmul_mx(
+                    out=acc[:],
+                    lhsT=codes[:].bitcast(FP8X4),
+                    lhsT_scale=scales[:],
+                    rhs=key_words[:, half(h)].bitcast(FP8X4),
+                    rhs_scale=key_scales[:, half(h)],
+                    start=True,
+                    stop=True,
+                )
+                banks.append(acc)
+            return banks
+
+        q_codes, q_scales = quantize("q", interleave(nc.vector.tensor_copy, "q_bf", q_raw, Q), Q)
+
+        boost_ps = bank("boost_ps", "D0")
+        for c in range(PACK):
+            nc.tensor.transpose(boost_ps[:, block(c)], boost_cols[:, c : c + 1].to_broadcast([P, P]), ident[:])
+        boost_view = boost_ps[:].rearrange("p (c n) -> p n c", c=PACK)
+        boost_b = tile("boost_b", [P, I])
+        nc.scalar.copy(out=boost_b[:].rearrange("p (n c) -> p n c", c=PACK), in_=boost_view)
+        neg_steep = tile("neg_steep", [P, 1])
+        nc.vector.tensor_scalar(neg_steep[:], steep_col[:], -1.0, None, ALU.mult)
+        half_steep = tile("half_steep", [P, 1])
+        nc.vector.tensor_scalar(half_steep[:], steep_col[:], 0.5, None, ALU.mult)
+        neg_qsteep = tile("neg_qsteep", [P, 1])
+        nc.vector.tensor_scalar(neg_qsteep[:], steep_col[:], -0.25, None, ALU.mult)
+
+        a_ps = score("a_ps", "A", q_codes, q_scales)
+        a = tile("a", [P, T])
+        nc.scalar.copy(out=a[:, half(0)], in_=a_ps[0][:])
+        nc.vector.tensor_copy(out=a[:, half(1)], in_=a_ps[1][:])
+        probe = tile("probe", [P, 2])
+        nc.gpsimd.tensor_copy(probe[:], a[:, 511:513])
+        a_g = tile("a_g", [P, I])
+        th = tile("th", [P, I])
+        b = tile("b", [P, I])
+        for r in range(RUNS):
+            nc.vector.tensor_copy(a_g[:, run(r)], a[:].indirect(offsets[:, run_cols(r)]))
+            nc.scalar.activation(th[:, run(r)], a_g[:, run(r)], ACT.Tanh, scale=half_steep[:])
+            nc.scalar.activation(b[:, run(r)], th[:, run(r)], ACT.Identity, scale=0.5, bias=0.5)
+
+        dq_codes, dq_scales = quantize("dq", interleave(nc.vector.tensor_copy, "dq_bf", dq_raw, Q), Q)
+        ta_ps = score("ta_ps", "B", dq_codes, dq_scales)
+
+        for r in range(RUNS):
+            nc.vector.tensor_tensor(bf[:].indirect(offsets[:, run_cols(r)]), b[:, run(r)], boost_b[:, run(r)], ALU.mult)
+
+        sq = tile("sq", [P, I])
+        nc.scalar.activation(sq[:], th[:], ACT.Square)
+        neg_sb = tile("neg_sb", [P, I])
+        nc.scalar.activation(neg_sb[:].rearrange("p (n c) -> p n c", c=PACK), boost_view, ACT.Copy, scale=neg_qsteep[:])
+        ta = tile("ta", [P, T])
+        for h in range(HALVES):
+            nc.scalar.copy(out=ta[:, half(h)], in_=ta_ps[h][:])
+
+        s = tile("s", [P, T])
+        nc.vector.tensor_tensor(s[:], a[:], bf[:], ALU.add)
+        neg_max = tile("neg_max", [P, 1])
+        nc.vector.tensor_reduce(neg_max[:], s[:], AXIS.X, ALU.max, negate=True)
+
+        v_bf = []
+        for c in range(CHUNKS):
+            v_bf.append(interleave(nc.scalar.copy, "v_bf%d" % c, v_raw[c], CHUNK))
+        g_bf = interleave(nc.scalar.copy, "g_bf", g_raw, Q)
+
+        p = tile("p", [P, T])
+        z = tile("z", [P, 1])
+        nc.scalar.activation(p[:], s[:], ACT.Exp, bias=neg_max[:], accum_out=z[:])
+
+        slope = tile("slope", [P, I])
+        nc.vector.scalar_tensor_tensor(slope[:], sq[:], 1.0, neg_sb[:], ALU.subtract, ALU.mult)
+        xbb = tile("xbb", [P, I])
+        nc.vector.tensor_tensor(xbb[:], ta[:].indirect(offsets[:]), slope[:], ALU.mult)
+
+        g_codes, g_scales = quantize("g", g_bf, Q)
+        v_q = [quantize("v%d" % c, v_bf[c], CHUNK) for c in range(CHUNKS)]
+
+        fac_ps = bank("fac_ps", "D1")
+        nc.tensor.transpose(fac_ps[:, 0:P], fac_rows[:], ident[:])
+        fac_cols = tile("fac_cols", [P, BLOCKS])
+        nc.scalar.copy(out=fac_cols[:], in_=fac_ps[:, 0:BLOCKS])
+
+        ct_ps = [bank("ct_ps%d" % h, "C%d" % h) for h in range(HALVES)]
+        for j in range(BLOCKS):
+            codes, scales = v_q[j * P // CHUNK]
+            cols = block(j % (CHUNK // P))
+            nc.tensor.matmul_mx(
+                out=ct_ps[j // PER_BANK][:, block(j % PER_BANK)],
+                lhsT=codes[:, cols].bitcast(FP8X4),
+                lhsT_scale=scales[:, cols],
+                rhs=g_codes[:].bitcast(FP8X4),
+                rhs_scale=g_scales[:],
+                start=True,
+                stop=True,
+            )
+        gt = tile("gt", [P, T])
+        for j in range(BLOCKS):
+            nc.scalar.activation(gt[:, block(j)], ct_ps[j // PER_BANK][:, block(j % PER_BANK)], ACT.Copy, scale=fac_cols[:, j : j + 1])
+        g_ps = [bank("g_ps%d" % h, "D%d" % h) for h in range(HALVES)]
+        for j in range(BLOCKS):
+            nc.tensor.transpose(g_ps[j // PER_BANK][:, block(j % PER_BANK)], gt[:, block(j)], ident[:])
+
+        curve = tile("curve", [P, I])
+        nc.vector.scalar_tensor_tensor(curve[:], th[:], neg_steep[:], xbb[:], ALU.mult, ALU.mult)
+
+        nc.vector.tensor_copy(xbf[:].indirect(offsets[:]), xbb[:])
+        xs = tile("xs", [P, T])
+        nc.gpsimd.tensor_tensor(xs[:], ta[:], xbf[:], ALU.add)
+
+        rz = tile("rz", [P, 1])
+        nc.vector.reciprocal(rz[:], z[:])
+        prob = tile("prob", [P, T])
+        nc.scalar.activation(prob[:], p[:], ACT.Copy, scale=rz[:])
+        neg_prob = tile("neg_prob", [P, T])
+        nc.scalar.activation(neg_prob[:], prob[:], ACT.Copy, scale=-1.0)
+
+        spent = tile("spent", [P, T])
+        m_part = [tile("m_part%d" % h, [P, 1]) for h in range(HALVES)]
+        for h in range(HALVES):
+            nc.vector.scalar_tensor_tensor(spent[:, half(h)], g_ps[h][:], 1.0, p[:, half(h)], ALU.mult, ALU.mult, accum_out=m_part[h][:])
+        m = tile("m", [P, 1])
+        nc.vector.tensor_scalar(m[:], m_part[0][:], m_part[1][:], rz[:], ALU.add, ALU.mult)
+        ds = tile("ds", [P, T])
+        for h in range(HALVES):
+            nc.vector.scalar_tensor_tensor(ds[:, half(h)], g_ps[h][:], m[:], prob[:, half(h)], ALU.subtract, ALU.mult)
+        mu = tile("mu", [P, 1])
+        spent2 = tile("spent2", [P, T])
+        nc.vector.scalar_tensor_tensor(spent2[:], xs[:], 1.0, prob[:], ALU.mult, ALU.mult, accum_out=mu[:])
+        v_term = tile("v_term", [P, I])
+        nc.vector.tensor_tensor(v_term[:], ds[:].indirect(offsets[:]), curve[:], ALU.mult)
+        hh = tile("hh", [P, T])
+        nu = tile("nu", [P, 1])
+        nc.vector.scalar_tensor_tensor(hh[:], xs[:], mu[:], ds[:], ALU.subtract, ALU.mult, accum_out=nu[:])
+        xds = tile("xds", [P, T])
+        nc.vector.scalar_tensor_tensor(xds[:], neg_prob[:], nu[:], hh[:], ALU.mult, ALU.add)
+        u_term = tile("u_term", [P, I])
+        nc.vector.tensor_tensor(u_term[:], xds[:].indirect(offsets[:]), slope[:], ALU.mult)
+        nc.vector.tensor_tensor(xs1[:].indirect(offsets[:]), u_term[:], v_term[:], ALU.add)
+
+        base_s = tile("base_s", [P, T])
+        nc.scalar.activation(base_s[:], base_sb[:], ACT.Copy, scale=1.0 / GAIN)
+        yt_ps = [bank("yt_ps%d" % h, "A%d" % h) for h in range(HALVES)]
+        for j in range(BLOCKS):
+            nc.tensor.matmul(yt_ps[j // PER_BANK][:, block(j % PER_BANK)], lhsT=base_s[:, block(j)], rhs=ident[:], is_transpose=True, start=(j % PER_BANK == 0), stop=False)
+        for j in range(BLOCKS):
+            nc.tensor.matmul(yt_ps[j // PER_BANK][:, block(j % PER_BANK)], lhsT=xds[:, block(j)], rhs=ident[:], is_transpose=True, start=False, stop=(j % PER_BANK == PER_BANK - 1))
+        yt = tile("yt", [P, T])
+        y0_ps = [bank("y0_ps%d" % h, "B%d" % h) for h in range(HALVES)]
+        for h in range(HALVES):
+            nc.scalar.activation(yt[:, half(h)], yt_ps[h][:], ACT.Copy, scale=GAIN)
+        for j in range(BLOCKS):
+            nc.tensor.transpose(y0_ps[j // PER_BANK][:, block(j % PER_BANK)], yt[:, block(j)], ident[:])
+
+        width = T // STORES
+        for c in range(STORES):
+            cols = slice(c * width, (c + 1) * width)
+            h = c * width // BANK
+            y = tile("y%d" % c, [P, width])
+            nc.vector.scalar_tensor_tensor(y[:], xs1[:, cols], GAIN, y0_ps[h][:, c * width - h * BANK : (c + 1) * width - h * BANK], ALU.mult, ALU.add)
+            nc.sync.dma_start(out=out[:, cols], in_=y[:])

@@ -36,8 +36,8 @@ def tile_attend_hvboost_heads_kernel(tc, query, keys_words, keys_scales, gout, v
         sb = ctx.enter_context(tc.tile_pool(name="sb", bufs=1))
         ps = ctx.enter_context(tc.psum_pool(name="ps", bufs=1))
 
-        def tile(name, shape, dtype=F32):
-            return sb.tile(shape, dtype, name=name, align_bytes=64)
+        def tile(name, shape, dtype=F32, tag=None):
+            return sb.tile(shape, dtype, name=name, tag=tag or name, align_bytes=64)
 
         def bank(name, tag):
             return ps.tile([P, BANK], F32, name=name, tag=tag)
@@ -61,22 +61,20 @@ def tile_attend_hvboost_heads_kernel(tc, query, keys_words, keys_scales, gout, v
         fac_rows = tile("fac_rows", [P, P])
         nc.vector.memset(fac_rows[:], 0.0)
         warm = tile("warm", [P, 8])
-        nc.vector.memset(warm[:], 0.0)
-        bf = tile("bf", [P, T])
-        xbf = tile("xbf", [P, T])
-        xs1 = tile("xs1", [P, T])
-        for w_ in (bf, xbf, xs1):
-            nc.vector.memset(w_[:], 0.0)
+        nc.gpsimd.memset(warm[:], 0.0)
+        placed = tile("placed", [P, T])
+        nc.vector.memset(placed[:], 0.0)
+        bf = xbf = xs1 = placed
 
         def load_rows(name, src, width):
             raw = tile(name, [P, PACK, width])
             nc.sync.dma_start(out=raw[:], in_=src.rearrange("(p j) w -> p j w", j=PACK))
             return raw
 
-        boost_cols = tile("boost_cols", [P, PACK])
-        nc.scalar.dma_start(out=boost_cols[:], in_=boost.rearrange("o (p c) -> p (o c)", c=PACK))
+        ident = tile("ident", [P, P])
+        make_identity(nc, ident[:])
         steep_col = tile("steep_col", [P, 1])
-        nc.scalar.dma_start(out=steep_col[:], in_=steep)
+        nc.gpsimd.dma_start(out=steep_col[:], in_=steep)
 
         q_raw = load_rows("q_raw", query, Q)
         key_words = tile("key_words", [P, T], U32)
@@ -86,8 +84,10 @@ def tile_attend_hvboost_heads_kernel(tc, query, keys_words, keys_scales, gout, v
                 out=key_scales[32 * quad : 32 * quad + 4, :].bitcast(I32),
                 in_=keys_scales[0, 4 * quad : 4 * quad + 4, :].bitcast(I32),
             )
-        nc.sync.dma_start(offsets[:], offs)
+        boost_b = tile("boost_b", [P, I])
+        nc.sync.dma_start(out=boost_b[:], in_=boost[0].partition_broadcast(P))
         dq_raw = load_rows("dq_raw", dquery, Q)
+        nc.sync.dma_start(offsets[:], offs)
         v_raw = [load_rows("v_raw%d" % c, vals[:, c * CHUNK : (c + 1) * CHUNK], CHUNK) for c in range(2)]
         g_raw = load_rows("g_raw", gout, Q)
         v_raw = v_raw + [load_rows("v_raw%d" % c, vals[:, c * CHUNK : (c + 1) * CHUNK], CHUNK) for c in range(2, CHUNKS)]
@@ -95,24 +95,20 @@ def tile_attend_hvboost_heads_kernel(tc, query, keys_words, keys_scales, gout, v
         base_sb = tile("base_sb", [P, T])
         nc.sync.dma_start(out=base_sb[:], in_=base)
 
-        ident = tile("ident", [P, P])
-        make_identity(nc, ident[:])
-
         warm_out = tile("warm_out", [P, 8])
-        nc.scalar.activation(warm_out[:, 0:1], warm[:, 0:1], ACT.Tanh)
+        nc.scalar.activation(warm_out[:, 0:1], warm[:, 0:1], ACT.Sigmoid)
 
-        def interleave(copy, name, raw, width):
-            grouped = tile(name, [P, width, PACK], BF16)
+        def interleave(copy, grouped, raw):
             copy(
-                out=grouped[:].rearrange("p (c i) j -> p c j i", i=4),
+                out=grouped.rearrange("p (c i) j -> p c j i", i=4),
                 in_=raw[:].rearrange("p j (c i) -> p c j i", i=4),
             )
             return grouped
 
-        def quantize(name, grouped, width):
-            codes = tile(name + "_codes", [P, width], U32)
+        def quantize(name, grouped, width, tag=None):
+            codes = tile(name + "_codes", [P, width], U32, tag=tag)
             scales = tile(name + "_scales", [P, width], U8)
-            nc.vector.quantize_mx(out=codes[:].bitcast(FP8X4), scales=scales[:], in_=grouped[:].rearrange("p w j -> p (w j)"))
+            nc.vector.quantize_mx(out=codes[:].bitcast(FP8X4), scales=scales[:], in_=grouped.rearrange("p w j -> p (w j)"))
             return codes, scales
 
         def score(name, tag, codes, scales):
@@ -131,100 +127,119 @@ def tile_attend_hvboost_heads_kernel(tc, query, keys_words, keys_scales, gout, v
                 banks.append(acc)
             return banks
 
-        q_codes, q_scales = quantize("q", interleave(nc.vector.tensor_copy, "q_bf", q_raw, Q), Q)
+        q_codes, q_scales = quantize("q", interleave(nc.vector.tensor_copy, tile("q_bf", [P, Q, PACK], BF16)[:], q_raw), Q)
 
-        boost_ps = bank("boost_ps", "D0")
-        for c in range(PACK):
-            nc.tensor.transpose(boost_ps[:, block(c)], boost_cols[:, c : c + 1].to_broadcast([P, P]), ident[:])
-        boost_view = boost_ps[:].rearrange("p (c n) -> p n c", c=PACK)
-        boost_b = tile("boost_b", [P, I])
-        nc.scalar.copy(out=boost_b[:].rearrange("p (n c) -> p n c", c=PACK), in_=boost_view)
         neg_steep = tile("neg_steep", [P, 1])
-        nc.vector.tensor_scalar(neg_steep[:], steep_col[:], -1.0, None, ALU.mult)
-        half_steep = tile("half_steep", [P, 1])
-        nc.vector.tensor_scalar(half_steep[:], steep_col[:], 0.5, None, ALU.mult)
-        neg_qsteep = tile("neg_qsteep", [P, 1])
-        nc.vector.tensor_scalar(neg_qsteep[:], steep_col[:], -0.25, None, ALU.mult)
+        nc.gpsimd.tensor_scalar(neg_steep[:], steep_col[:], -1.0, 0.0, ALU.mult, ALU.add)
+        neg2_steep = tile("neg2_steep", [P, 1])
+        nc.gpsimd.tensor_scalar(neg2_steep[:], steep_col[:], -2.0, 0.0, ALU.mult, ALU.add)
 
-        a_ps = score("a_ps", "A", q_codes, q_scales)
         a = tile("a", [P, T])
-        nc.scalar.copy(out=a[:, half(0)], in_=a_ps[0][:])
-        nc.vector.tensor_copy(out=a[:, half(1)], in_=a_ps[1][:])
-        probe = tile("probe", [P, 2])
-        nc.gpsimd.tensor_copy(probe[:], a[:, 511:513])
-        a_g = tile("a_g", [P, I])
-        th = tile("th", [P, I])
+        for c, tag in enumerate(("A0", "A1", "C0", "C1")):
+            cols = slice(c * CHUNK, (c + 1) * CHUNK)
+            acc = bank("a_ps%d" % c, tag)
+            nc.tensor.matmul_mx(
+                out=acc[:, 0:CHUNK],
+                lhsT=q_codes[:].bitcast(FP8X4),
+                lhsT_scale=q_scales[:],
+                rhs=key_words[:, cols].bitcast(FP8X4),
+                rhs_scale=key_scales[:, cols],
+                start=True,
+                stop=True,
+            )
+            (nc.vector.tensor_copy if c % 2 == 0 else nc.scalar.copy)(out=a[:, cols], in_=acc[:, 0:CHUNK])
+        a_g = [tile("a_g0", [P, I // RUNS]), tile("a_g1", [P, I // RUNS])]
         b = tile("b", [P, I])
         for r in range(RUNS):
-            nc.vector.tensor_copy(a_g[:, run(r)], a[:].indirect(offsets[:, run_cols(r)]))
-            nc.scalar.activation(th[:, run(r)], a_g[:, run(r)], ACT.Tanh, scale=half_steep[:])
-            nc.scalar.activation(b[:, run(r)], th[:, run(r)], ACT.Identity, scale=0.5, bias=0.5)
+            nc.vector.tensor_copy(a_g[r][:], a[:].indirect(offsets[:, run_cols(r)]))
+            nc.scalar.activation(b[:, run(r)], a_g[r][:], ACT.Sigmoid, scale=steep_col[:])
 
-        dq_codes, dq_scales = quantize("dq", interleave(nc.vector.tensor_copy, "dq_bf", dq_raw, Q), Q)
+        dq_codes, dq_scales = quantize("dq", interleave(nc.vector.tensor_copy, tile("dq_bf", [P, Q, PACK], BF16)[:], dq_raw), Q, tag="q_codes")
         ta_ps = score("ta_ps", "B", dq_codes, dq_scales)
 
         for r in range(RUNS):
             nc.vector.tensor_tensor(bf[:].indirect(offsets[:, run_cols(r)]), b[:, run(r)], boost_b[:, run(r)], ALU.mult)
 
         sq = tile("sq", [P, I])
-        nc.scalar.activation(sq[:], th[:], ACT.Square)
-        neg_sb = tile("neg_sb", [P, I])
-        nc.scalar.activation(neg_sb[:].rearrange("p (n c) -> p n c", c=PACK), boost_view, ACT.Copy, scale=neg_qsteep[:])
-        ta = tile("ta", [P, T])
+        nc.scalar.activation(sq[:], b[:], ACT.Square, bias=-0.5)
+        neg_sb = boost_b
+        nc.vector.tensor_scalar(neg_sb[:], boost_b[:], neg_steep[:], None, ALU.mult)
+        ta = tile("ta", [P, T], tag="a_g0")
         for h in range(HALVES):
             nc.scalar.copy(out=ta[:, half(h)], in_=ta_ps[h][:])
 
+        def turned_sum(name, tag, first, second):
+            banks = [bank("%s%d" % (name, h), "%s%d" % (tag, h)) for h in range(HALVES)]
+            for j in range(BLOCKS):
+                nc.tensor.matmul(banks[j // PER_BANK][:, block(j % PER_BANK)], lhsT=first[:, block(j)], rhs=ident[:], is_transpose=True, start=(j % PER_BANK == 0), stop=False)
+            for j in range(BLOCKS):
+                nc.tensor.matmul(banks[j // PER_BANK][:, block(j % PER_BANK)], lhsT=second[:, block(j)], rhs=ident[:], is_transpose=True, start=False, stop=(j % PER_BANK == PER_BANK - 1))
+            return banks
+
+        def turn(name, tag, src):
+            banks = [bank("%s%d" % (name, h), "%s%d" % (tag, h)) for h in range(HALVES)]
+            for j in range(BLOCKS):
+                nc.tensor.transpose(banks[j // PER_BANK][:, block(j % PER_BANK)], src[:, block(j)], ident[:])
+            return banks
+
         s = tile("s", [P, T])
         nc.vector.tensor_tensor(s[:], a[:], bf[:], ALU.add)
-        neg_max = tile("neg_max", [P, 1])
-        nc.vector.tensor_reduce(neg_max[:], s[:], AXIS.X, ALU.max, negate=True)
-
-        v_bf = []
-        for c in range(CHUNKS):
-            v_bf.append(interleave(nc.scalar.copy, "v_bf%d" % c, v_raw[c], CHUNK))
-        g_bf = interleave(nc.scalar.copy, "g_bf", g_raw, Q)
-
-        p = tile("p", [P, T])
-        z = tile("z", [P, 1])
-        nc.scalar.activation(p[:], s[:], ACT.Exp, bias=neg_max[:], accum_out=z[:])
-
         slope = tile("slope", [P, I])
-        nc.vector.scalar_tensor_tensor(slope[:], sq[:], 1.0, neg_sb[:], ALU.subtract, ALU.mult)
-        xbb = tile("xbb", [P, I])
-        nc.vector.tensor_tensor(xbb[:], ta[:].indirect(offsets[:]), slope[:], ALU.mult)
+        nc.vector.scalar_tensor_tensor(slope[:], sq[:], 0.25, neg_sb[:], ALU.subtract, ALU.mult)
+        neg_max = tile("neg_max", [P, 1])
+        neg_s = tile("neg_s", [P, T])
+        nc.vector.tensor_scalar(neg_s[:], s[:], -1.0, None, ALU.mult, ALU.min, accum_out=neg_max[:])
 
-        g_codes, g_scales = quantize("g", g_bf, Q)
-        v_q = [quantize("v%d" % c, v_bf[c], CHUNK) for c in range(CHUNKS)]
+        late_bf = tile("late_bf", [P, T + Q, PACK], BF16, tag="a_g1")
+        for c in range(CHUNKS):
+            if c == 2:
+                interleave(nc.scalar.copy, late_bf[:, T : T + Q, :], g_raw)
+            interleave(nc.scalar.copy, late_bf[:, c * CHUNK : (c + 1) * CHUNK, :], v_raw[c])
+        p = tile("p", [P, T], tag="v_raw3")
+        z = tile("z", [P, 1])
+        nc.scalar.activation(p[:], neg_s[:], ACT.Exp, bias=neg_max[:], scale=-1.0, accum_out=z[:])
+        def gather_times(name, window, factor, r, tag=None):
+            picked = tile(name, [P, I // RUNS], tag=tag)
+            nc.vector.tensor_tensor(picked[:], window[:].indirect(offsets[:, run_cols(r)]), factor[:, run(r)], ALU.mult)
+            return picked
 
-        fac_ps = bank("fac_ps", "D1")
+        bend = tile("bend", [P, I], tag="sq")
+        nc.gpsimd.tensor_scalar(bend[:], b[:], neg2_steep[:], steep_col[:], ALU.mult, ALU.add)
+        xbb = [gather_times("xbb0", ta, slope, 0)]
+        late_codes = tile("late_codes", [P, T + Q], U32, tag="s")
+        late_scales = tile("late_scales", [P, T + Q], U8)
+        g_cols = slice(T, T + Q)
+        for cols in (g_cols, half(0), half(1)):
+            nc.vector.quantize_mx(out=late_codes[:, cols].bitcast(FP8X4), scales=late_scales[:, cols], in_=late_bf[:, cols, :].rearrange("p w j -> p (w j)"))
+
+        xbb.append(gather_times("xbb1", ta, slope, 1, tag="a_g1"))
+
+        fac_ps = bank("fac_ps", "B0")
         nc.tensor.transpose(fac_ps[:, 0:P], fac_rows[:], ident[:])
-        fac_cols = tile("fac_cols", [P, BLOCKS])
+        fac_cols = tile("fac_cols", [P, BLOCKS], tag="neg_max")
         nc.scalar.copy(out=fac_cols[:], in_=fac_ps[:, 0:BLOCKS])
 
         ct_ps = [bank("ct_ps%d" % h, "C%d" % h) for h in range(HALVES)]
         for j in range(BLOCKS):
-            codes, scales = v_q[j * P // CHUNK]
-            cols = block(j % (CHUNK // P))
             nc.tensor.matmul_mx(
                 out=ct_ps[j // PER_BANK][:, block(j % PER_BANK)],
-                lhsT=codes[:, cols].bitcast(FP8X4),
-                lhsT_scale=scales[:, cols],
-                rhs=g_codes[:].bitcast(FP8X4),
-                rhs_scale=g_scales[:],
+                lhsT=late_codes[:, block(j)].bitcast(FP8X4),
+                lhsT_scale=late_scales[:, block(j)],
+                rhs=late_codes[:, g_cols].bitcast(FP8X4),
+                rhs_scale=late_scales[:, g_cols],
                 start=True,
                 stop=True,
             )
         gt = tile("gt", [P, T])
         for j in range(BLOCKS):
             nc.scalar.activation(gt[:, block(j)], ct_ps[j // PER_BANK][:, block(j % PER_BANK)], ACT.Copy, scale=fac_cols[:, j : j + 1])
-        g_ps = [bank("g_ps%d" % h, "D%d" % h) for h in range(HALVES)]
-        for j in range(BLOCKS):
-            nc.tensor.transpose(g_ps[j // PER_BANK][:, block(j % PER_BANK)], gt[:, block(j)], ident[:])
+        g_ps = turn("g_ps", "D", gt)
 
-        curve = tile("curve", [P, I])
-        nc.vector.scalar_tensor_tensor(curve[:], th[:], neg_steep[:], xbb[:], ALU.mult, ALU.mult)
 
-        nc.vector.tensor_copy(xbf[:].indirect(offsets[:]), xbb[:])
+        nc.vector.tensor_copy(xbf[:].indirect(offsets[:, run_cols(0)]), xbb[0][:])
+        curve0 = tile("curve0", [P, I // RUNS])
+        nc.vector.tensor_tensor(curve0[:], xbb[0][:], bend[:, run(0)], ALU.mult)
+        nc.vector.tensor_copy(xbf[:].indirect(offsets[:, run_cols(1)]), xbb[1][:])
         xs = tile("xs", [P, T])
         nc.gpsimd.tensor_tensor(xs[:], ta[:], xbf[:], ALU.add)
 
@@ -247,30 +262,27 @@ def tile_attend_hvboost_heads_kernel(tc, query, keys_words, keys_scales, gout, v
         mu = tile("mu", [P, 1])
         spent2 = tile("spent2", [P, T])
         nc.vector.scalar_tensor_tensor(spent2[:], xs[:], 1.0, prob[:], ALU.mult, ALU.mult, accum_out=mu[:])
-        v_term = tile("v_term", [P, I])
-        nc.vector.tensor_tensor(v_term[:], ds[:].indirect(offsets[:]), curve[:], ALU.mult)
+        curve1 = tile("curve1", [P, I // RUNS], tag="m_part0")
+        nc.vector.tensor_tensor(curve1[:], xbb[1][:], bend[:, run(1)], ALU.mult)
         hh = tile("hh", [P, T])
         nu = tile("nu", [P, 1])
         nc.vector.scalar_tensor_tensor(hh[:], xs[:], mu[:], ds[:], ALU.subtract, ALU.mult, accum_out=nu[:])
+        v_term = tile("v_term", [P, I])
+        nc.vector.tensor_tensor(v_term[:, run(0)], ds[:].indirect(offsets[:, run_cols(0)]), curve0[:], ALU.mult)
         xds = tile("xds", [P, T])
         nc.vector.scalar_tensor_tensor(xds[:], neg_prob[:], nu[:], hh[:], ALU.mult, ALU.add)
+        nc.vector.tensor_tensor(v_term[:, run(1)], ds[:].indirect(offsets[:, run_cols(1)]), curve1[:], ALU.mult)
         u_term = tile("u_term", [P, I])
         nc.vector.tensor_tensor(u_term[:], xds[:].indirect(offsets[:]), slope[:], ALU.mult)
         nc.vector.tensor_tensor(xs1[:].indirect(offsets[:]), u_term[:], v_term[:], ALU.add)
 
-        base_s = tile("base_s", [P, T])
+        base_s = tile("base_s", [P, T], tag="gt")
         nc.scalar.activation(base_s[:], base_sb[:], ACT.Copy, scale=1.0 / GAIN)
-        yt_ps = [bank("yt_ps%d" % h, "A%d" % h) for h in range(HALVES)]
-        for j in range(BLOCKS):
-            nc.tensor.matmul(yt_ps[j // PER_BANK][:, block(j % PER_BANK)], lhsT=base_s[:, block(j)], rhs=ident[:], is_transpose=True, start=(j % PER_BANK == 0), stop=False)
-        for j in range(BLOCKS):
-            nc.tensor.matmul(yt_ps[j // PER_BANK][:, block(j % PER_BANK)], lhsT=xds[:, block(j)], rhs=ident[:], is_transpose=True, start=False, stop=(j % PER_BANK == PER_BANK - 1))
+        yt_ps = turned_sum("yt_ps", "A", base_s, xds)
         yt = tile("yt", [P, T])
-        y0_ps = [bank("y0_ps%d" % h, "B%d" % h) for h in range(HALVES)]
         for h in range(HALVES):
             nc.scalar.activation(yt[:, half(h)], yt_ps[h][:], ACT.Copy, scale=GAIN)
-        for j in range(BLOCKS):
-            nc.tensor.transpose(y0_ps[j // PER_BANK][:, block(j % PER_BANK)], yt[:, block(j)], ident[:])
+        y0_ps = turn("y0_ps", "B", yt)
 
         width = T // STORES
         for c in range(STORES):
@@ -278,4 +290,4 @@ def tile_attend_hvboost_heads_kernel(tc, query, keys_words, keys_scales, gout, v
             h = c * width // BANK
             y = tile("y%d" % c, [P, width])
             nc.vector.scalar_tensor_tensor(y[:], xs1[:, cols], GAIN, y0_ps[h][:, c * width - h * BANK : (c + 1) * width - h * BANK], ALU.mult, ALU.add)
-            nc.sync.dma_start(out=out[:, cols], in_=y[:])
+            (nc.sync if c % 2 == 0 else nc.scalar).dma_start(out=out[:, cols], in_=y[:])

@@ -73,8 +73,10 @@ def tile_attend_hvboost_heads_kernel(tc, query, keys_words, keys_scales, gout, v
 
         ident = tile("ident", [P, P])
         make_identity(nc, ident[:])
+        boost_cols = tile("boost_cols", [P, PACK])
+        nc.scalar.dma_start(out=boost_cols[:], in_=boost.rearrange("o (p c) -> p (o c)", c=PACK))
         steep_col = tile("steep_col", [P, 1])
-        nc.gpsimd.dma_start(out=steep_col[:], in_=steep)
+        nc.scalar.dma_start(out=steep_col[:], in_=steep)
 
         q_raw = load_rows("q_raw", query, Q)
         key_words = tile("key_words", [P, T], U32)
@@ -84,8 +86,6 @@ def tile_attend_hvboost_heads_kernel(tc, query, keys_words, keys_scales, gout, v
                 out=key_scales[32 * quad : 32 * quad + 4, :].bitcast(I32),
                 in_=keys_scales[0, 4 * quad : 4 * quad + 4, :].bitcast(I32),
             )
-        boost_b = tile("boost_b", [P, I])
-        nc.sync.dma_start(out=boost_b[:], in_=boost[0].partition_broadcast(P))
         dq_raw = load_rows("dq_raw", dquery, Q)
         nc.sync.dma_start(offsets[:], offs)
         v_raw = [load_rows("v_raw%d" % c, vals[:, c * CHUNK : (c + 1) * CHUNK], CHUNK) for c in range(2)]
@@ -127,7 +127,12 @@ def tile_attend_hvboost_heads_kernel(tc, query, keys_words, keys_scales, gout, v
                 banks.append(acc)
             return banks
 
-        q_codes, q_scales = quantize("q", interleave(nc.vector.tensor_copy, tile("q_bf", [P, Q, PACK], BF16)[:], q_raw), Q)
+        boost_ps = bank("boost_ps", "D0")
+        for c in range(PACK):
+            nc.tensor.transpose(boost_ps[:, block(c)], boost_cols[:, c : c + 1].to_broadcast([P, P]), ident[:])
+        boost_b = tile("boost_b", [P, I])
+        nc.scalar.copy(out=boost_b[:].rearrange("p (n c) -> p n c", c=PACK), in_=boost_ps[:].rearrange("p (c n) -> p n c", c=PACK))
+        q_codes, q_scales = quantize("q", interleave(nc.vector.tensor_copy, tile("q_bf", [P, Q, PACK], BF16)[:], q_raw), Q, tag="boost_cols")
 
         neg_steep = tile("neg_steep", [P, 1])
         nc.gpsimd.tensor_scalar(neg_steep[:], steep_col[:], -1.0, 0.0, ALU.mult, ALU.add)
@@ -154,7 +159,7 @@ def tile_attend_hvboost_heads_kernel(tc, query, keys_words, keys_scales, gout, v
             nc.vector.tensor_copy(a_g[r][:], a[:].indirect(offsets[:, run_cols(r)]))
             nc.scalar.activation(b[:, run(r)], a_g[r][:], ACT.Sigmoid, scale=steep_col[:])
 
-        dq_codes, dq_scales = quantize("dq", interleave(nc.vector.tensor_copy, tile("dq_bf", [P, Q, PACK], BF16)[:], dq_raw), Q, tag="q_codes")
+        dq_codes, dq_scales = quantize("dq", interleave(nc.vector.tensor_copy, tile("dq_bf", [P, Q, PACK], BF16)[:], dq_raw), Q, tag="boost_cols")
         ta_ps = score("ta_ps", "B", dq_codes, dq_scales)
 
         for r in range(RUNS):

@@ -88,9 +88,8 @@ def tile_attend_hvboost_heads_kernel(tc, query, keys_words, keys_scales, gout, v
             )
         dq_raw = load_rows("dq_raw", dquery, Q)
         nc.sync.dma_start(offsets[:], offs)
-        v_raw = [load_rows("v_raw%d" % c, vals[:, c * CHUNK : (c + 1) * CHUNK], CHUNK) for c in range(2)]
         g_raw = load_rows("g_raw", gout, Q)
-        v_raw = v_raw + [load_rows("v_raw%d" % c, vals[:, c * CHUNK : (c + 1) * CHUNK], CHUNK) for c in range(2, CHUNKS)]
+        v_raw = [load_rows("v_raw%d" % c, vals[:, c * CHUNK : (c + 1) * CHUNK], CHUNK) for c in range(CHUNKS)]
         nc.sync.dma_start(out=fac_rows[0:BLOCKS, :], in_=fac.rearrange("o (j p) -> (o j) p", p=P))
         base_sb = tile("base_sb", [P, T])
         nc.sync.dma_start(out=base_sb[:], in_=base)
@@ -100,8 +99,8 @@ def tile_attend_hvboost_heads_kernel(tc, query, keys_words, keys_scales, gout, v
 
         def interleave(copy, grouped, raw):
             copy(
-                out=grouped.rearrange("p (c i) j -> p c j i", i=4),
-                in_=raw[:].rearrange("p j (c i) -> p c j i", i=4),
+                out=grouped.rearrange("p (c i) j -> p c j i", i=2),
+                in_=raw[:].rearrange("p j (c i) -> p c j i", i=2),
             )
             return grouped
 
@@ -162,6 +161,7 @@ def tile_attend_hvboost_heads_kernel(tc, query, keys_words, keys_scales, gout, v
         dq_codes, dq_scales = quantize("dq", interleave(nc.vector.tensor_copy, tile("dq_bf", [P, Q, PACK], BF16)[:], dq_raw), Q, tag="boost_cols")
         ta_ps = score("ta_ps", "B", dq_codes, dq_scales)
 
+        g_bf = interleave(nc.scalar.copy, tile("g_bf", [P, Q, PACK], BF16, tag="dq_bf")[:], g_raw)
         for r in range(RUNS):
             nc.vector.tensor_tensor(bf[:].indirect(offsets[:, run_cols(r)]), b[:, run(r)], boost_b[:, run(r)], ALU.mult)
 
@@ -195,10 +195,8 @@ def tile_attend_hvboost_heads_kernel(tc, query, keys_words, keys_scales, gout, v
         neg_s = tile("neg_s", [P, T])
         nc.vector.tensor_scalar(neg_s[:], s[:], -1.0, None, ALU.mult, ALU.min, accum_out=neg_max[:])
 
-        late_bf = tile("late_bf", [P, T + Q, PACK], BF16, tag="a_g1")
+        late_bf = tile("late_bf", [P, T, PACK], BF16, tag="a_g1")
         for c in range(CHUNKS):
-            if c == 2:
-                interleave(nc.scalar.copy, late_bf[:, T : T + Q, :], g_raw)
             interleave(nc.scalar.copy, late_bf[:, c * CHUNK : (c + 1) * CHUNK, :], v_raw[c])
         p = tile("p", [P, T], tag="v_raw3")
         z = tile("z", [P, 1])
@@ -214,8 +212,8 @@ def tile_attend_hvboost_heads_kernel(tc, query, keys_words, keys_scales, gout, v
         late_codes = tile("late_codes", [P, T + Q], U32, tag="s")
         late_scales = tile("late_scales", [P, T + Q], U8)
         g_cols = slice(T, T + Q)
-        for cols in (g_cols, half(0), half(1)):
-            nc.vector.quantize_mx(out=late_codes[:, cols].bitcast(FP8X4), scales=late_scales[:, cols], in_=late_bf[:, cols, :].rearrange("p w j -> p (w j)"))
+        for cols, grouped in ((g_cols, g_bf), (half(0), late_bf[:, half(0), :]), (half(1), late_bf[:, half(1), :])):
+            nc.vector.quantize_mx(out=late_codes[:, cols].bitcast(FP8X4), scales=late_scales[:, cols], in_=grouped.rearrange("p w j -> p (w j)"))
 
         xbb.append(gather_times("xbb1", ta, slope, 1, tag="a_g1"))
 
@@ -248,9 +246,9 @@ def tile_attend_hvboost_heads_kernel(tc, query, keys_words, keys_scales, gout, v
         xs = tile("xs", [P, T])
         nc.gpsimd.tensor_tensor(xs[:], ta[:], xbf[:], ALU.add)
 
-        rz = tile("rz", [P, 1])
+        rz = tile("rz", [P, 1], tag="xbb0")
         nc.vector.reciprocal(rz[:], z[:])
-        prob = tile("prob", [P, T])
+        prob = tile("prob", [P, T], tag="neg_max")
         nc.scalar.activation(prob[:], p[:], ACT.Copy, scale=rz[:])
         neg_prob = tile("neg_prob", [P, T])
         nc.scalar.activation(neg_prob[:], prob[:], ACT.Copy, scale=-1.0)
@@ -267,7 +265,7 @@ def tile_attend_hvboost_heads_kernel(tc, query, keys_words, keys_scales, gout, v
         mu = tile("mu", [P, 1])
         spent2 = tile("spent2", [P, T])
         nc.vector.scalar_tensor_tensor(spent2[:], xs[:], 1.0, prob[:], ALU.mult, ALU.mult, accum_out=mu[:])
-        curve1 = tile("curve1", [P, I // RUNS], tag="m_part0")
+        curve1 = tile("curve1", [P, I // RUNS], tag="m")
         nc.vector.tensor_tensor(curve1[:], xbb[1][:], bend[:, run(1)], ALU.mult)
         hh = tile("hh", [P, T])
         nu = tile("nu", [P, 1])

from contextlib import ExitStack

import concourse.mybir as mybir
from concourse.masks import make_identity

F32 = mybir.dt.float32
BF16 = mybir.dt.bfloat16
I32 = mybir.dt.int32
U32 = mybir.dt.uint32
U16 = mybir.dt.uint16
U8 = mybir.dt.uint8
FP8X4 = mybir.dt.float8_e4m3fn_x4
ALU = mybir.AluOpType
ACT = mybir.ActivationFunctionType
AXIS = mybir.AxisListType

P = 128
PACK = 4
D, E, T, Q, I = 512, 512, 1024, 128, 512
BANK = 512
HALVES = T // BANK
BLOCKS = T // P
PER_BANK = BANK // P
CHUNK = 256
CHUNKS = T // CHUNK
GAIN = 1024.0
STORES = 4
RUNS = 2

FLOPS = 3 * 2 * 512 * Q * T


def tile_attend_hvboost_heads_kernel(tc, query, keys_words, keys_scales, gout, vals, steep, boost, fac, dquery, base, offs, out):
    nc = tc.nc
    with ExitStack() as ctx:
        sb = ctx.enter_context(tc.tile_pool(name="sb", bufs=1))
        ps = ctx.enter_context(tc.psum_pool(name="ps", bufs=1))

        def tile(name, shape, dtype=F32, tag=None):
            return sb.tile(shape, dtype, name=name, tag=tag or name, align_bytes=64)

        def bank(name, tag):
            return ps.tile([P, BANK], F32, name=name, tag=tag)

        def half(h):
            return slice(h * BANK, (h + 1) * BANK)

        def block(j):
            return slice(j * P, (j + 1) * P)

        def run(r):
            return slice(r * I // RUNS, (r + 1) * I // RUNS)

        def run_cols(r):
            return slice(r * I // RUNS // 16, (r + 1) * I // RUNS // 16)

        offsets = sb.tile([P, I // 16], U16, name="offsets")

        key_scales = tile("key_scales", [P, T], U8)
        nc.gpsimd.memset(key_scales[:].bitcast(I32), 0)
        fac_rows = tile("fac_rows", [P, P])
        nc.vector.memset(fac_rows[:], 0.0)
        warm = tile("warm", [P, 8])
        nc.gpsimd.memset(warm[:], 0.0)
        placed = tile("placed", [P, T])
        nc.vector.memset(placed[:], 0.0)
        bf = xbf = xs1 = placed

        def load_rows(name, src, width):
            raw = tile(name, [P, PACK, width])
            nc.sync.dma_start(out=raw[:], in_=src.rearrange("(p j) w -> p j w", j=PACK))
            return raw

        ident = tile("ident", [P, P])
        make_identity(nc, ident[:])
        boost_cols = tile("boost_cols", [P, PACK])
        nc.scalar.dma_start(out=boost_cols[:], in_=boost.rearrange("o (p c) -> p (o c)", c=PACK))
        steep_col = tile("steep_col", [P, 1])
        nc.scalar.dma_start(out=steep_col[:], in_=steep)

        q_raw = load_rows("q_raw", query, Q)
        key_words = tile("key_words", [P, T], U32)
        nc.sync.dma_start(out=key_words[:].bitcast(I32), in_=keys_words[0].rearrange("p n t -> p (n t)").bitcast(I32))
        for quad in range(4):
            nc.scalar.dma_start(
                out=key_scales[32 * quad : 32 * quad + 4, :].bitcast(I32),
                in_=keys_scales[0, 4 * quad : 4 * quad + 4, :].bitcast(I32),
            )
        dq_raw = load_rows("dq_raw", dquery, Q)
        nc.sync.dma_start(offsets[:], offs)
        g_raw = load_rows("g_raw", gout, Q)
        v_raw = [load_rows("v_raw%d" % c, vals[:, c * CHUNK : (c + 1) * CHUNK], CHUNK) for c in range(CHUNKS)]
        nc.sync.dma_start(out=fac_rows[0:BLOCKS, :], in_=fac.rearrange("o (j p) -> (o j) p", p=P))
        base_sb = tile("base_sb", [P, T])
        nc.sync.dma_start(out=base_sb[:], in_=base)

        warm_out = tile("warm_out", [P, 8])
        nc.scalar.activation(warm_out[:, 0:1], warm[:, 0:1], ACT.Sigmoid)

        def interleave(copy, grouped, raw):
            copy(
                out=grouped.rearrange("p (c i) j -> p c j i", i=2),
                in_=raw[:].rearrange("p j (c i) -> p c j i", i=2),
            )
            return grouped

        def quantize(name, grouped, width, tag=None):
            codes = tile(name + "_codes", [P, width], U32, tag=tag)
            scales = tile(name + "_scales", [P, width], U8)
            nc.vector.quantize_mx(out=codes[:].bitcast(FP8X4), scales=scales[:], in_=grouped.rearrange("p w j -> p (w j)"))
            return codes, scales

        def score(name, tag, codes, scales):
            banks = []
            for h in range(HALVES):
                acc = bank("%s%d" % (name, h), "%s%d" % (tag, h))
                nc.tensor.matmul_mx(
                    out=acc[:],
                    lhsT=codes[:].bitcast(FP8X4),
                    lhsT_scale=scales[:],
                    rhs=key_words[:, half(h)].bitcast(FP8X4),
                    rhs_scale=key_scales[:, half(h)],
                    start=True,
                    stop=True,
                )
                banks.append(acc)
            return banks

        boost_ps = bank("boost_ps", "D0")
        for c in range(PACK):
            nc.tensor.transpose(boost_ps[:, block(c)], boost_cols[:, c : c + 1].to_broadcast([P, P]), ident[:])
        boost_b = tile("boost_b", [P, I])
        nc.scalar.copy(out=boost_b[:].rearrange("p (n c) -> p n c", c=PACK), in_=boost_ps[:].rearrange("p (c n) -> p n c", c=PACK))
        q_codes, q_scales = quantize("q", interleave(nc.vector.tensor_copy, tile("q_bf", [P, Q, PACK], BF16)[:], q_raw), Q, tag="boost_cols")

        neg_steep = tile("neg_steep", [P, 1])
        nc.gpsimd.tensor_scalar(neg_steep[:], steep_col[:], -1.0, 0.0, ALU.mult, ALU.add)
        neg2_steep = tile("neg2_steep", [P, 1])
        nc.gpsimd.tensor_scalar(neg2_steep[:], steep_col[:], -2.0, 0.0, ALU.mult, ALU.add)

        a = tile("a", [P, T])
        for c, tag in enumerate(("A0", "A1", "C0", "C1")):
            cols = slice(c * CHUNK, (c + 1) * CHUNK)
            acc = bank("a_ps%d" % c, tag)
            nc.tensor.matmul_mx(
                out=acc[:, 0:CHUNK],
                lhsT=q_codes[:].bitcast(FP8X4),
                lhsT_scale=q_scales[:],
                rhs=key_words[:, cols].bitcast(FP8X4),
                rhs_scale=key_scales[:, cols],
                start=True,
                stop=True,
            )
            (nc.vector.tensor_copy if c % 2 == 0 else nc.scalar.copy)(out=a[:, cols], in_=acc[:, 0:CHUNK])
        a_g = [tile("a_g0", [P, I // RUNS]), tile("a_g1", [P, I // RUNS])]
        b = tile("b", [P, I])
        for r in range(RUNS):
            nc.vector.tensor_copy(a_g[r][:], a[:].indirect(offsets[:, run_cols(r)]))
            nc.scalar.activation(b[:, run(r)], a_g[r][:], ACT.Sigmoid, scale=steep_col[:])

        dq_codes, dq_scales = quantize("dq", interleave(nc.vector.tensor_copy, tile("dq_bf", [P, Q, PACK], BF16)[:], dq_raw), Q, tag="boost_cols")
        ta_ps = score("ta_ps", "B", dq_codes, dq_scales)

        g_bf = interleave(nc.scalar.copy, tile("g_bf", [P, Q, PACK], BF16, tag="dq_bf")[:], g_raw)
        for r in range(RUNS):
            nc.vector.tensor_tensor(bf[:].indirect(offsets[:, run_cols(r)]), b[:, run(r)], boost_b[:, run(r)], ALU.mult)

        sq = tile("sq", [P, I])
        nc.scalar.activation(sq[:], b[:], ACT.Square, bias=-0.5)
        neg_sb = boost_b
        nc.vector.tensor_scalar(neg_sb[:], boost_b[:], neg_steep[:], None, ALU.mult)
        ta = tile("ta", [P, T], tag="a_g0")
        for h in range(HALVES):
            nc.scalar.copy(out=ta[:, half(h)], in_=ta_ps[h][:])

        def turned_sum(name, tag, first, second):
            banks = [bank("%s%d" % (name, h), "%s%d" % (tag, h)) for h in range(HALVES)]
            for j in range(BLOCKS):
                nc.tensor.matmul(banks[j // PER_BANK][:, block(j % PER_BANK)], lhsT=first[:, block(j)], rhs=ident[:], is_transpose=True, start=(j % PER_BANK == 0), stop=False)
            for j in range(BLOCKS):
                nc.tensor.matmul(banks[j // PER_BANK][:, block(j % PER_BANK)], lhsT=second[:, block(j)], rhs=ident[:], is_transpose=True, start=False, stop=(j % PER_BANK == PER_BANK - 1))
            return banks

        def turn(name, tag, src):
            banks = [bank("%s%d" % (name, h), "%s%d" % (tag, h)) for h in range(HALVES)]
            for j in range(BLOCKS):
                nc.tensor.transpose(banks[j // PER_BANK][:, block(j % PER_BANK)], src[:, block(j)], ident[:])
            return banks

        s = tile("s", [P, T])
        nc.vector.tensor_tensor(s[:], a[:], bf[:], ALU.add)
        slope = tile("slope", [P, I])
        nc.vector.scalar_tensor_tensor(slope[:], sq[:], 0.25, neg_sb[:], ALU.subtract, ALU.mult)
        neg_max = tile("neg_max", [P, 1])
        neg_s = tile("neg_s", [P, T])
        nc.vector.tensor_scalar(neg_s[:], s[:], -1.0, None, ALU.mult, ALU.min, accum_out=neg_max[:])

        late_bf = tile("late_bf", [P, T, PACK], BF16, tag="a_g1")
        for c in range(CHUNKS):
            interleave(nc.scalar.copy, late_bf[:, c * CHUNK : (c + 1) * CHUNK, :], v_raw[c])
        p = tile("p", [P, T], tag="v_raw3")
        z = tile("z", [P, 1])
        nc.scalar.activation(p[:], neg_s[:], ACT.Exp, bias=neg_max[:], scale=-1.0, accum_out=z[:])
        def gather_times(name, window, factor, r, tag=None):
            picked = tile(name, [P, I // RUNS], tag=tag)
            nc.vector.tensor_tensor(picked[:], window[:].indirect(offsets[:, run_cols(r)]), factor[:, run(r)], ALU.mult)
            return picked

        bend = tile("bend", [P, I], tag="sq")
        nc.gpsimd.tensor_scalar(bend[:], b[:], neg2_steep[:], steep_col[:], ALU.mult, ALU.add)
        xbb = [gather_times("xbb0", ta, slope, 0)]
        late_codes = tile("late_codes", [P, T + Q], U32, tag="s")
        late_scales = tile("late_scales", [P, T + Q], U8)
        g_cols = slice(T, T + Q)
        for cols, grouped in ((g_cols, g_bf), (half(0), late_bf[:, half(0), :]), (half(1), late_bf[:, half(1), :])):
            nc.vector.quantize_mx(out=late_codes[:, cols].bitcast(FP8X4), scales=late_scales[:, cols], in_=grouped.rearrange("p w j -> p (w j)"))

        xbb.append(gather_times("xbb1", ta, slope, 1, tag="a_g1"))

        fac_ps = bank("fac_ps", "B0")
        nc.tensor.transpose(fac_ps[:, 0:P], fac_rows[:], ident[:])
        fac_cols = tile("fac_cols", [P, BLOCKS], tag="neg_max")
        nc.scalar.copy(out=fac_cols[:], in_=fac_ps[:, 0:BLOCKS])

        ct_ps = [bank("ct_ps%d" % h, "C%d" % h) for h in range(HALVES)]
        for j in range(BLOCKS):
            nc.tensor.matmul_mx(
                out=ct_ps[j // PER_BANK][:, block(j % PER_BANK)],
                lhsT=late_codes[:, block(j)].bitcast(FP8X4),
                lhsT_scale=late_scales[:, block(j)],
                rhs=late_codes[:, g_cols].bitcast(FP8X4),
                rhs_scale=late_scales[:, g_cols],
                start=True,
                stop=True,
            )
        gt = tile("gt", [P, T])
        for j in range(BLOCKS):
            nc.scalar.activation(gt[:, block(j)], ct_ps[j // PER_BANK][:, block(j % PER_BANK)], ACT.Copy, scale=fac_cols[:, j : j + 1])
        g_ps = turn("g_ps", "D", gt)


        nc.vector.tensor_copy(xbf[:].indirect(offsets[:, run_cols(0)]), xbb[0][:])
        curve0 = tile("curve0", [P, I // RUNS])
        nc.vector.tensor_tensor(curve0[:], xbb[0][:], bend[:, run(0)], ALU.mult)
        nc.vector.tensor_copy(xbf[:].indirect(offsets[:, run_cols(1)]), xbb[1][:])
        xs = tile("xs", [P, T])
        nc.gpsimd.tensor_tensor(xs[:], ta[:], xbf[:], ALU.add)

        rz = tile("rz", [P, 1], tag="xbb0")
        nc.vector.reciprocal(rz[:], z[:])
        prob = tile("prob", [P, T], tag="neg_max")
        nc.scalar.activation(prob[:], p[:], ACT.Copy, scale=rz[:])
        neg_prob = tile("neg_prob", [P, T])
        nc.scalar.activation(neg_prob[:], prob[:], ACT.Copy, scale=-1.0)

        spent = tile("spent", [P, T])
        m_part = [tile("m_part%d" % h, [P, 1]) for h in range(HALVES)]
        for h in range(HALVES):
            nc.vector.scalar_tensor_tensor(spent[:, half(h)], g_ps[h][:], 1.0, p[:, half(h)], ALU.mult, ALU.mult, accum_out=m_part[h][:])
        m = tile("m", [P, 1])
        nc.vector.tensor_scalar(m[:], m_part[0][:], m_part[1][:], rz[:], ALU.add, ALU.mult)
        ds = tile("ds", [P, T])
        for h in range(HALVES):
            nc.vector.scalar_tensor_tensor(ds[:, half(h)], g_ps[h][:], m[:], prob[:, half(h)], ALU.subtract, ALU.mult)
        mu = tile("mu", [P, 1])
        spent2 = tile("spent2", [P, T])
        nc.vector.scalar_tensor_tensor(spent2[:], xs[:], 1.0, prob[:], ALU.mult, ALU.mult, accum_out=mu[:])
        curve1 = tile("curve1", [P, I // RUNS], tag="m")
        nc.vector.tensor_tensor(curve1[:], xbb[1][:], bend[:, run(1)], ALU.mult)
        hh = tile("hh", [P, T])
        nu = tile("nu", [P, 1])
        nc.vector.scalar_tensor_tensor(hh[:], xs[:], mu[:], ds[:], ALU.subtract, ALU.mult, accum_out=nu[:])
        v_term = tile("v_term", [P, I])
        nc.vector.tensor_tensor(v_term[:, run(0)], ds[:].indirect(offsets[:, run_cols(0)]), curve0[:], ALU.mult)
        xds = tile("xds", [P, T])
        nc.vector.scalar_tensor_tensor(xds[:], neg_prob[:], nu[:], hh[:], ALU.mult, ALU.add)
        nc.vector.tensor_tensor(v_term[:, run(1)], ds[:].indirect(offsets[:, run_cols(1)]), curve1[:], ALU.mult)
        u_term = tile("u_term", [P, I])
        nc.vector.tensor_tensor(u_term[:], xds[:].indirect(offsets[:]), slope[:], ALU.mult)
        nc.vector.tensor_tensor(xs1[:].indirect(offsets[:]), u_term[:], v_term[:], ALU.add)

        base_s = tile("base_s", [P, T], tag="gt")
        nc.scalar.activation(base_s[:], base_sb[:], ACT.Copy, scale=1.0 / GAIN)
        yt_ps = turned_sum("yt_ps", "A", base_s, xds)
        yt = tile("yt", [P, T])
        for h in range(HALVES):
            nc.scalar.activation(yt[:, half(h)], yt_ps[h][:], ACT.Copy, scale=GAIN)
        y0_ps = turn("y0_ps", "B", yt)

        width = T // STORES
        for c in range(STORES):
            cols = slice(c * width, (c + 1) * width)
            h = c * width // BANK
            y = tile("y%d" % c, [P, width])
            nc.vector.scalar_tensor_tensor(y[:], xs1[:, cols], GAIN, y0_ps[h][:, c * width - h * BANK : (c + 1) * width - h * BANK], ALU.mult, ALU.add)
            (nc.sync if c % 2 == 0 else nc.scalar).dma_start(out=out[:, cols], in_=y[:])
